import numpy as np
import ml_dtypes


def mxq(x, axis, fmt="e4m3"):
    dtype, down = {"e4m3": (ml_dtypes.float8_e4m3fn, 7), "e5m2": (ml_dtypes.float8_e5m2, 14)}[fmt]
    v = np.moveaxis(np.asarray(x, np.float32).astype(ml_dtypes.bfloat16).astype(np.float64), axis, -1)
    blocks = v.reshape(v.shape[:-1] + (-1, 32))
    amax = np.abs(blocks).max(-1, keepdims=True)
    byte = np.maximum(np.where(amax > 0, np.frexp(amax)[1] - 1 + 127, 0) - down, 1)
    scale = np.exp2(byte - 127.0)
    codes = (blocks / scale).astype(np.float32).astype(dtype).astype(np.float64)
    return np.moveaxis((codes * scale).reshape(v.shape), -1, axis)


WIDE = False


def mx_kscale(k):
    if not WIDE:
        return np.ones(k)
    levels = np.array([30, -30])
    if k % 512:
        return np.exp2(np.random.permutation(np.resize(levels, k // 32))).repeat(32)
    a = np.empty((k // 512, 16))
    for p in range(k // 512):
        a[p, :8] = np.random.permutation(np.resize(levels, 8))
        for g in range(8):
            far = levels[np.abs(levels - a[p, g]) >= 10]
            a[p, g + 8] = far[np.random.randint(len(far))]
    return np.exp2(a.ravel()).repeat(32)


def f64(x):
    return np.asarray(x).astype(np.float64)


def striped(idx):
    return np.tile(np.asarray(idx).reshape(-1, 16).T, (8, 1)).astype(np.uint16)


def unstriped(offs):
    return offs[:16].T.reshape(-1).astype(np.int64)


E2M1 = np.array([0.0, 0.5, 1.0, 1.5, 2.0, 3.0, 4.0, 6.0, -0.0, -0.5, -1.0, -1.5, -2.0, -3.0, -4.0, -6.0])


def pack_weight(w, fmt):
    k, n = w.shape
    w = f64(np.asarray(w, np.float32).astype(ml_dtypes.bfloat16)).reshape(k // 32, 32, n)
    amax = np.abs(w).max(1)
    if fmt in ("e4m3", "e5m2"):
        byte = np.frexp(amax)[1] - 1 + 127 - (7 if fmt == "e4m3" else 14)
    else:
        mant, ex = np.frexp(amax / 6.0)
        byte = np.where(mant > 0.5, ex, ex - 1) + 127
    byte = np.clip(np.where(amax > 0, byte, 1), 1, 254)
    scaled = (w * np.exp2(127.0 - byte)[:, None, :]).reshape(k, n).astype(np.float32)
    by_word = np.ascontiguousarray(scaled.reshape(k // 512, 128, 4, n).transpose(0, 1, 3, 2))
    if fmt in ("e4m3", "e5m2"):
        words = by_word.astype(ml_dtypes.float8_e4m3fn if fmt == "e4m3" else ml_dtypes.float8_e5m2).view(np.uint8)
    else:
        c = by_word.astype(ml_dtypes.float4_e2m1fn).view(np.uint8) & 0xF
        words = (c[..., 0::2] | (c[..., 1::2] << 4)).reshape(k // 512, 128, 2 * n)
    return np.ascontiguousarray(words), np.ascontiguousarray(byte.astype(np.uint8).reshape(k // 512, 16, n))


def unpack_weight(words, scales, fmt):
    g, _, n = scales.shape
    words = np.ascontiguousarray(words).reshape(g, 128, n, -1)
    if fmt in ("e4m3", "e5m2"):
        vals = words.view(ml_dtypes.float8_e4m3fn if fmt == "e4m3" else ml_dtypes.float8_e5m2).astype(np.float64)
    else:
        nib = np.empty((g, 128, n, 4), np.uint8)
        nib[..., 0::2] = words & 0xF
        nib[..., 1::2] = words >> 4
        vals = E2M1[nib]
    vals = vals * np.repeat(np.exp2(scales.astype(np.float64) - 127.0), 8, axis=1)[..., None]
    return vals.transpose(0, 1, 3, 2).reshape(g * 512, n)


K, F, T, Z, J, R, C, N, L, E = 512, 512, 1024, 1024, 256, 512, 512, 256, 512, 1024


def setup_inputs():
    n = np.random.standard_normal
    idx = np.random.permutation(T)[:J]
    idx2 = np.random.permutation(Z)[:J]
    idx3 = np.random.permutation(C)[:J]
    idx4 = np.random.permutation(C)[:J]
    idx5 = np.random.permutation(E)[:J]
    fk = mx_kscale(K)
    fr = mx_kscale(R)
    ff = mx_kscale(F)
    fl = mx_kscale(L)
    xtp = pack_weight(n((K, T)) / fk[:, None], "e2m1")
    wp = pack_weight(n((K, R)) * 1 / np.sqrt(K) * fk[:, None] * fr, "e5m2")
    xop = pack_weight(n((F, Z)) / ff[:, None], "e5m2")
    w2p = pack_weight(n((F, R)) * 1 / np.sqrt(F) * ff[:, None] * fr, "e4m3")
    wbp = pack_weight(n((R, N)) * 1 / np.sqrt(R) / fr[:, None], "e4m3")
    sxp = pack_weight(n((L, J)) / fl[:, None], "e5m2")
    wsp = pack_weight(n((L, N)) * 1 / np.sqrt(L) * fl[:, None], "e4m3")
    return {
        "xt_words": xtp[0],
        "xt_scales": xtp[1],
        "w_words": wp[0],
        "w_scales": wp[1],
        "xo_words": xop[0],
        "xo_scales": xop[1],
        "w2_words": w2p[0],
        "w2_scales": w2p[1],
        "wb_words": wbp[0],
        "wb_scales": wbp[1],
        "sx_words": sxp[0],
        "sx_scales": sxp[1],
        "ws_words": wsp[0],
        "ws_scales": wsp[1],
        "offs": striped(idx),
        "offs2": striped(idx2),
        "offs3": striped(idx3),
        "offs4": striped(idx4),
        "offs5": striped(idx5),
    }


def reference(xt_words, xt_scales, w_words, w_scales, xo_words, xo_scales, w2_words, w2_scales, wb_words, wb_scales, sx_words, sx_scales, ws_words, ws_scales, offs, offs2, offs3, offs4, offs5):
    idx = unstriped(offs)
    idx2 = unstriped(offs2)
    idx3 = unstriped(offs3)
    idx4 = unstriped(offs4)
    idx5 = unstriped(offs5)
    xtu = unpack_weight(xt_words, xt_scales, "e2m1")
    wu = unpack_weight(w_words, w_scales, "e5m2")
    xou = unpack_weight(xo_words, xo_scales, "e5m2")
    w2u = unpack_weight(w2_words, w2_scales, "e4m3")
    wbu = unpack_weight(wb_words, wb_scales, "e4m3")
    sxu = unpack_weight(sx_words, sx_scales, "e5m2")
    wsu = unpack_weight(ws_words, ws_scales, "e4m3")
    xtidxg = xtu[:, idx]
    a = wu.T @ xtidxg
    xoidx2g = xou[:, idx2]
    b = w2u.T @ xoidx2g
    pw = np.zeros((R, C))
    pw[:, idx3] = a
    hid = np.abs(pw[:, idx4] - b)
    hidq = mxq(hid, 0, "e5m2")
    p = wbu.T @ hidq + wsu.T @ sxu
    y = np.zeros((N, E))
    y[:, idx5] = p
    return y

from contextlib import ExitStack

import concourse.mybir as mybir

K, T, Z, J, R, C, N, E = 512, 1024, 1024, 256, 512, 512, 256, 1024
FLOPS = 2 * J * (2 * K * R + 2 * R * N)

F32 = mybir.dt.float32
BF16 = mybir.dt.bfloat16
I32 = mybir.dt.int32
U32 = mybir.dt.uint32
U16 = mybir.dt.uint16
U8 = mybir.dt.uint8
E4M3 = mybir.dt.float8_e4m3fn_x4
E5M2 = mybir.dt.float8_e5m2_x4
E2M1 = mybir.dt.float4_e2m1fn_x4
COPY = mybir.ActivationFunctionType.Copy
ABS = mybir.ActivationFunctionType.Abs

P = 128
PACK = 4
HALVES = 2
JH = J // HALVES
LIST_COLS = J // 16


def tile_list_twotab_board_skip_scattered_kernel(
    tc, xt_words, xt_scales, w_words, w_scales, xo_words, xo_scales, w2_words, w2_scales,
    wb_words, wb_scales, sx_words, sx_scales, ws_words, ws_scales, offs, offs2, offs3, offs4, offs5, out,
):
    nc = tc.nc

    with ExitStack() as ctx:
        sb = ctx.enter_context(tc.tile_pool(name="sb", bufs=1))
        ps = ctx.enter_context(tc.psum_pool(name="ps", bufs=1))

        def tile(name, shape, dtype):
            return sb.tile(shape, dtype, name=name, align_bytes=64)

        def load_list(name, src):
            lst = tile(name, [P, LIST_COLS], U16)
            nc.sync.dma_start(lst[:], src)
            return lst

        def load_words(name, src, cols, dtype):
            words = tile(name, [P, cols], dtype)
            nc.sync.dma_start(words[:].bitcast(I32), src.bitcast(I32))
            return words

        def fp8_rows(src):
            return src[0].rearrange("p n t -> p (n t)")

        def load_scales(plane, col0, src):
            cols = src.shape[2]
            for q in range(4):
                nc.sync.dma_start(
                    plane[32 * q : 32 * q + 4, col0 : col0 + cols].bitcast(I32),
                    src[0, 4 * q : 4 * q + 4, :].bitcast(I32),
                )

        def zeroed_plane(name, cols):
            plane = tile(name, [P, cols], U8)
            nc.vector.memset(plane[:].bitcast(I32), 0)
            return plane

        def deal_words(name, raw):
            dealt = tile(name, [P, R], U32)
            nc.scalar.copy(
                dealt[:].rearrange("p (t c i) -> p c t i", t=PACK, i=4),
                raw[:].rearrange("p (c i t) -> p c t i", t=PACK, i=4),
            )
            return dealt

        def deal_scales(name, raw):
            dealt = tile(name, [P, R], U8)
            nc.vector.tensor_copy(
                dealt[:].rearrange("p (t m) -> p t m", t=PACK),
                raw.rearrange("p (m t) -> p t m", t=PACK),
            )
            return dealt

        def gather(name, window, lst, dtype):
            picked = tile(name, [P, J], dtype)
            nc.vector.tensor_copy(picked[:], window[:].indirect(lst[:]))
            return picked

        def move(on_scalar, dst, src):
            if on_scalar:
                nc.scalar.activation(dst, src, COPY)
            else:
                nc.vector.tensor_copy(dst, src)

        xt_plane = zeroed_plane("xt_plane", T)
        w_plane = zeroed_plane("w_plane", R)
        xo_plane = zeroed_plane("xo_plane", Z)
        late_plane = zeroed_plane("late_plane", R + N + J + N)
        w2_col, ws_col, sx_col, wb_col = 0, R, R + N, R + N + J

        idx = load_list("idx", offs)
        xt_raw = load_words("xt_raw", xt_words[0], T, U16)
        w_raw = load_words("w_raw", fp8_rows(w_words), R, U32)
        load_scales(xt_plane, 0, xt_scales)
        load_scales(w_plane, 0, w_scales)
        idx2 = load_list("idx2", offs2)
        xo_raw = load_words("xo_raw", fp8_rows(xo_words), Z, U32)
        idx3 = load_list("idx3", offs3)
        load_scales(xo_plane, 0, xo_scales)
        w2_raw = load_words("w2_raw", fp8_rows(w2_words), R, U32)
        load_scales(late_plane, w2_col, w2_scales)
        idx4 = load_list("idx4", offs4)
        ws_codes = load_words("ws_codes", fp8_rows(ws_words), N, U32)
        sx_codes = load_words("sx_codes", fp8_rows(sx_words), J, U32)
        wb_codes = load_words("wb_codes", fp8_rows(wb_words), N, U32)
        load_scales(late_plane, ws_col, ws_scales)
        load_scales(late_plane, sx_col, sx_scales)
        load_scales(late_plane, wb_col, wb_scales)
        idx5 = load_list("idx5", offs5)

        boards = []
        for t in range(PACK):
            board = tile("board%d" % t, [P, C], F32)
            nc.vector.memset(board[:], 0.0)
            boards.append(board)

        w_codes = deal_words("w_codes", w_raw)
        xt_codes = gather("xt_codes", xt_raw, idx, U16)
        xt_exps = gather("xt_exps", xt_plane, idx, U8)
        w_exps = deal_scales("w_exps", w_plane[:])

        a_rows = []
        for t in (1, 0, 3, 2):
            cols = slice(P * t, P * (t + 1))
            a_ps = ps.tile([P, J], F32, name="a_ps%d" % t, tag="acc%d" % t)
            nc.tensor.matmul_mx(
                out=a_ps[:], lhsT=w_codes[:, cols].bitcast(E5M2), lhsT_scale=w_exps[:, cols],
                rhs=xt_codes[:].bitcast(E2M1), rhs_scale=xt_exps[:], start=True, stop=True,
            )
            a_rows.append((t, a_ps))

        xo_codes = gather("xo_codes", xo_raw, idx2, U32)
        xo_exps = gather("xo_exps", xo_plane, idx2, U8)
        w2_exps = deal_scales("w2_exps", late_plane[:, w2_col : w2_col + R])

        for pair in (a_rows[:2], a_rows[2:]):
            staged = []
            for t, a_ps in pair:
                a_sb = tile("a_sb%d" % t, [P, J], F32)
                nc.scalar.activation(a_sb[:], a_ps[:], COPY)
                staged.append((t, a_sb))
            for t, a_sb in staged:
                move(t % 2 == 0, boards[t][:].indirect(idx3[:]), a_sb[:])

        w2_codes = deal_words("w2_codes", w2_raw)

        pages = []
        for m in range(N // P):
            page = tile("page%d" % m, [P, E], F32)
            nc.vector.memset(page[:], 0.0)
            pages.append(page)

        b_ps = []
        for h in range(HALVES):
            slots = slice(JH * h, JH * (h + 1))
            bank = ps.tile([P, PACK, JH], F32, name="b_ps%d" % h)
            for t in range(PACK):
                cols = slice(P * t, P * (t + 1))
                nc.tensor.matmul_mx(
                    out=bank[:, t, :], lhsT=w2_codes[:, cols].bitcast(E4M3), lhsT_scale=w2_exps[:, cols],
                    rhs=xo_codes[:, slots].bitcast(E5M2), rhs_scale=xo_exps[:, slots], start=True, stop=True,
                )
            b_ps.append(bank)

        p_ps = {}
        for h in range(HALVES):
            for m in range(N // P):
                acc = ps.tile([P, JH], F32, name="p_ps%d%d" % (h, m), tag="acc%d" % (2 * h + m))
                nc.tensor.matmul_mx(
                    out=acc[:], lhsT=ws_codes[:, P * m : P * (m + 1)].bitcast(E4M3),
                    lhsT_scale=late_plane[:, ws_col + P * m : ws_col + P * (m + 1)],
                    rhs=sx_codes[:, JH * h : JH * (h + 1)].bitcast(E5M2),
                    rhs_scale=late_plane[:, sx_col + JH * h : sx_col + JH * (h + 1)], start=True, stop=False,
                )
                p_ps[h, m] = acc

        hids = []
        for h in range(HALVES):
            entries = slice(JH // 16 * h, JH // 16 * (h + 1))
            read = tile("read%d" % h, [P, PACK, JH], F32)
            for t in range(PACK):
                move(t % 2 == 0, read[:, t, :], boards[t][:].indirect(idx4[:, entries]))
            diff = tile("diff%d" % h, [P, PACK, JH], F32)
            nc.vector.tensor_tensor(diff[:], read[:], b_ps[h][:], mybir.AluOpType.subtract)
            hid = tile("hid%d" % h, [P, JH, PACK], BF16)
            nc.scalar.activation(
                hid[:].rearrange("p (c i) t -> p c t i", i=4),
                diff[:].rearrange("p t (c i) -> p c t i", i=4),
                ABS,
            )
            hids.append(hid)

        for h in range(HALVES):
            entries = slice(JH // 16 * h, JH // 16 * (h + 1))
            hid_codes = tile("hid_codes%d" % h, [P, JH], U32)
            hid_exps = tile("hid_exps%d" % h, [P, JH], U8)
            nc.vector.quantize_mx(
                out=hid_codes[:].bitcast(E5M2), scales=hid_exps[:],
                in_=hids[h][:].rearrange("p j t -> p (j t)"),
            )
            for m in range(N // P):
                nc.tensor.matmul_mx(
                    out=p_ps[h, m][:], lhsT=wb_codes[:, P * m : P * (m + 1)].bitcast(E4M3),
                    lhsT_scale=late_plane[:, wb_col + P * m : wb_col + P * (m + 1)],
                    rhs=hid_codes[:].bitcast(E5M2), rhs_scale=hid_exps[:], start=False, stop=True,
                )
        for h in range(HALVES):
            entries = slice(JH // 16 * h, JH // 16 * (h + 1))
            for m in range(N // P):
                p_sb = tile("p_sb%d%d" % (h, m), [P, JH], F32)
                move(m == 0, p_sb[:], p_ps[h, m][:])
                move(m == 0, pages[m][:].indirect(idx5[:, entries]), p_sb[:])

        for m in range(N // P):
            nc.sync.dma_start(out[P * m : P * (m + 1), :], pages[m][:])
